import numpy as np
import ml_dtypes


def mxq(x, axis, fmt="e4m3"):
    dtype, down = {"e4m3": (ml_dtypes.float8_e4m3fn, 7), "e5m2": (ml_dtypes.float8_e5m2, 14)}[fmt]
    v = np.moveaxis(np.asarray(x, np.float32).astype(ml_dtypes.bfloat16).astype(np.float64), axis, -1)
    blocks = v.reshape(v.shape[:-1] + (-1, 32))
    amax = np.abs(blocks).max(-1, keepdims=True)
    byte = np.maximum(np.where(amax > 0, np.frexp(amax)[1] - 1 + 127, 0) - down, 1)
    scale = np.exp2(byte - 127.0)
    codes = (blocks / scale).astype(np.float32).astype(dtype).astype(np.float64)
    return np.moveaxis((codes * scale).reshape(v.shape), -1, axis)


WIDE = False


def mx_kscale(k):
    if not WIDE:
        return np.ones(k)
    levels = np.array([10, -10, 5, -5, 0])
    if k % 512:
        return np.exp2(np.random.permutation(np.resize(levels, k // 32))).repeat(32)
    a = np.empty((k // 512, 16))
    for p in range(k // 512):
        a[p, :8] = np.random.permutation(np.resize(levels, 8))
        for g in range(8):
            far = levels[np.abs(levels - a[p, g]) >= 10]
            a[p, g + 8] = far[np.random.randint(len(far))]
    return np.exp2(a.ravel()).repeat(32)


def f64(x):
    return np.asarray(x).astype(np.float64)


def striped(idx):
    return np.tile(np.asarray(idx).reshape(-1, 16).T, (8, 1)).astype(np.uint16)


def unstriped(offs):
    return offs[:16].T.reshape(-1).astype(np.int64)


E2M1 = np.array([0.0, 0.5, 1.0, 1.5, 2.0, 3.0, 4.0, 6.0, -0.0, -0.5, -1.0, -1.5, -2.0, -3.0, -4.0, -6.0])


def pack_weight(w, fmt):
    k, n = w.shape
    w = f64(np.asarray(w, np.float32).astype(ml_dtypes.bfloat16)).reshape(k // 32, 32, n)
    amax = np.abs(w).max(1)
    if fmt == "e4m3":
        byte = np.frexp(amax)[1] - 1 + 127 - 7
    else:
        mant, ex = np.frexp(amax / 6.0)
        byte = np.where(mant > 0.5, ex, ex - 1) + 127
    byte = np.clip(np.where(amax > 0, byte, 1), 1, 254)
    scaled = (w * np.exp2(127.0 - byte)[:, None, :]).reshape(k, n).astype(np.float32)
    by_word = np.ascontiguousarray(scaled.reshape(k // 512, 128, 4, n).transpose(0, 1, 3, 2))
    if fmt == "e4m3":
        words = by_word.astype(ml_dtypes.float8_e4m3fn).view(np.uint8)
    else:
        c = by_word.astype(ml_dtypes.float4_e2m1fn).view(np.uint8) & 0xF
        words = (c[..., 0::2] | (c[..., 1::2] << 4)).reshape(k // 512, 128, 2 * n)
    return np.ascontiguousarray(words), np.ascontiguousarray(byte.astype(np.uint8).reshape(k // 512, 16, n))


def unpack_weight(words, scales, fmt):
    g, _, n = scales.shape
    words = np.ascontiguousarray(words).reshape(g, 128, n, -1)
    if fmt == "e4m3":
        vals = words.view(ml_dtypes.float8_e4m3fn).astype(np.float64)
    else:
        nib = np.empty((g, 128, n, 4), np.uint8)
        nib[..., 0::2] = words & 0xF
        nib[..., 1::2] = words >> 4
        vals = E2M1[nib]
    vals = vals * np.repeat(np.exp2(scales.astype(np.float64) - 127.0), 8, axis=1)[..., None]
    return vals.transpose(0, 1, 3, 2).reshape(g * 512, n)


def silu(v):
    return v / (1.0 + np.exp(-v))


K, T, U, V, J, L, N = 512, 1024, 1024, 1024, 512, 512, 512


def setup_inputs():
    n = np.random.standard_normal
    idx = np.random.permutation(T)[:J]
    idx2 = np.random.permutation(U)[:J]
    idx3 = np.random.permutation(V)[:J]
    fk = mx_kscale(K)
    fl = mx_kscale(L)
    wp = pack_weight(n((K, N)) * 1 / np.sqrt(K) * fk[:, None], "e2m1")
    dxp = pack_weight(n((L, J)) / fl[:, None], "e4m3")
    wdp = pack_weight(n((L, N)) * 1 / np.sqrt(L) * fl[:, None], "e2m1")
    return {
        "xa": (n((K, T))).astype(np.float32),
        "xb": (n((K, U))).astype(np.float32),
        "xc": (n((K, V))).astype(np.float32),
        "fk": (np.random.uniform(0.5, 2.0, (K, 1)) / fk[:, None]).astype(np.float32),
        "w_words": wp[0],
        "w_scales": wp[1],
        "dx_words": dxp[0],
        "dx_scales": dxp[1],
        "wd_words": wdp[0],
        "wd_scales": wdp[1],
        "offs": striped(idx),
        "offs2": striped(idx2),
        "offs3": striped(idx3),
    }


def reference(xa, xb, xc, fk, w_words, w_scales, dx_words, dx_scales, wd_words, wd_scales, offs, offs2, offs3):
    idx = unstriped(offs)
    idx2 = unstriped(offs2)
    idx3 = unstriped(offs3)
    wu = unpack_weight(w_words, w_scales, "e2m1")
    dxu = unpack_weight(dx_words, dx_scales, "e4m3")
    wdu = unpack_weight(wd_words, wd_scales, "e2m1")
    s = (f64(xa)[:, idx] + f64(xb)[:, idx2] + f64(xc)[:, idx3]) * f64(fk)
    sq = mxq(s, 0, "e4m3")
    z = wu.T @ sq + wdu.T @ dxu
    y = silu(0.6 * z)
    return y

@@ -1,0 +1,131 @@
+from contextlib import ExitStack
+
+import concourse.mybir as mybir
+
+K, T, J, L, N = 512, 1024, 512, 512, 512
+FLOPS = 2 * K * N * J + 2 * L * N * J
+
+F32 = mybir.dt.float32
+BF16 = mybir.dt.bfloat16
+I32 = mybir.dt.int32
+U32 = mybir.dt.uint32
+U16 = mybir.dt.uint16
+U8 = mybir.dt.uint8
+FP8X4 = mybir.dt.float8_e4m3fn_x4
+FP4X4 = mybir.dt.float4_e2m1fn_x4
+ADD = mybir.AluOpType.add
+COPY = mybir.ActivationFunctionType.Copy
+SILU = mybir.ActivationFunctionType.Silu
+
+P = 128
+PACK = 4
+LIST_ROWS = 16
+SLICE = 128
+SLICES = J // SLICE
+BLOCKS = N // P
+
+ORDER = [(0, 0), (0, 1), (1, 0), (1, 1), (2, 0), (0, 2), (2, 1), (1, 2), (0, 3), (2, 2), (1, 3), (2, 3)]
+
+
+def tile_list_three_tables_summed_kernel(
+    tc, xa, xb, xc, fk, w_words, w_scales, dx_words, dx_scales, wd_words, wd_scales, offs, offs2, offs3, out
+):
+    nc = tc.nc
+    with ExitStack() as ctx:
+        keep = ctx.enter_context(tc.tile_pool(name="keep", bufs=1))
+        psum = ctx.enter_context(tc.psum_pool(name="psum", bufs=1))
+
+        sources = [x.rearrange("(p t) c -> p t c", t=PACK) for x in (xa, xb, xc)]
+        lists_in = [offs, offs2, offs3]
+        lists = [keep.tile([P, J // LIST_ROWS], U16, name="list%d" % i) for i in range(3)]
+        planes = {(i, t): keep.tile([P, T], F32, name="plane%d_%d" % (i, t)) for i, t in ORDER}
+        sums = {(i, t): keep.tile([P, J], F32, name="sum%d_%d" % (i, t)) for i, t in ORDER}
+        factor = keep.tile([P, PACK], F32, name="factor")
+        w_codes = keep.tile([P, 2 * N], U8, name="w_codes", align_bytes=64)
+        wd_codes = keep.tile([P, 2 * N], U8, name="wd_codes", align_bytes=64)
+        dx_codes = keep.tile([P, J], U32, name="dx_codes", align_bytes=64)
+        given_scales = keep.tile([P, 3, N], U8, name="given_scales", align_bytes=64)
+        grouped = keep.tile([P, J, PACK], BF16, name="grouped", align_bytes=64)
+        s_codes = keep.tile([P, J], U32, name="s_codes", align_bytes=64)
+        s_scales = keep.tile([P, J], U8, name="s_scales", align_bytes=64)
+        w_sc, wd_sc, dx_sc = given_scales[:, 0, :], given_scales[:, 1, :], given_scales[:, 2, :]
+
+        nc.vector.memset(given_scales[:].rearrange("p a n -> p (a n)").bitcast(U32), 0)
+        scale_rows = [(a, src, q) for a, src in enumerate((w_scales, wd_scales, dx_scales)) for q in range(4)]
+
+        for step, (i, t) in enumerate(ORDER):
+            if step == len(ORDER) - 1:
+                nc.sync.dma_start(wd_codes[:].bitcast(I32), wd_words[0].bitcast(I32))
+                nc.sync.dma_start(
+                    dx_codes[:].bitcast(I32), dx_words[0].rearrange("p n t -> p (n t)").bitcast(I32)
+                )
+            nc.sync.dma_start(planes[i, t][:], sources[i][:, t, :])
+            if t == 0:
+                nc.sync.dma_start(lists[i][:], lists_in[i])
+            if (i, t) == (2, 0):
+                nc.sync.dma_start(factor[:], fk.rearrange("(p t) o -> p (t o)", t=PACK))
+            if step >= 5:
+                for a, src, q in scale_rows[2 * (step - 5) : 2 * (step - 4)]:
+                    nc.sync.dma_start(
+                        given_scales[32 * q : 32 * q + 4, a, :].bitcast(I32),
+                        src[0, 4 * q : 4 * q + 4, :].bitcast(I32),
+                    )
+        nc.sync.dma_start(w_codes[:].bitcast(I32), w_words[0].bitcast(I32))
+
+        def gather(i, t, j0, j1):
+            picked = planes[i, t][:].indirect(lists[i][:, j0 // LIST_ROWS : j1 // LIST_ROWS])
+            if i == 0:
+                nc.vector.tensor_copy(sums[i, t][:, j0:j1], picked)
+            else:
+                nc.vector.tensor_tensor(sums[i, t][:, j0:j1], picked, sums[i - 1, t][:, j0:j1], ADD)
+
+        def scale_and_group(t, j0, j1):
+            nc.scalar.activation(grouped[:, j0:j1, t], sums[2, t][:, j0:j1], COPY, scale=factor[:, t : t + 1])
+
+        banks = [psum.tile([P, BLOCKS, SLICE], F32, name="bank%d" % q) for q in range(SLICES)]
+
+        for i, t in ORDER[:-2]:
+            gather(i, t, 0, J)
+            if i == 2:
+                scale_and_group(t, 0, J)
+        gather(1, 3, 0, J // 2)
+        gather(1, 3, J // 2, J)
+
+        for q in range(SLICES):
+            cols = slice(q * SLICE, (q + 1) * SLICE)
+            for b in range(BLOCKS):
+                nc.tensor.matmul_mx(
+                    out=banks[q][:, b, :],
+                    lhsT=wd_codes[:, 2 * P * b : 2 * P * (b + 1)].bitcast(FP4X4),
+                    lhsT_scale=wd_sc[:, P * b : P * (b + 1)],
+                    rhs=dx_codes[:, cols].bitcast(FP8X4),
+                    rhs_scale=dx_sc[:, cols],
+                    start=(b == 0),
+                    stop=False,
+                )
+
+        for q in range(SLICES):
+            gather(2, 3, q * SLICE, (q + 1) * SLICE)
+            scale_and_group(3, q * SLICE, (q + 1) * SLICE)
+
+        out_rows = out.rearrange("(b p) j -> p b j", p=P)
+        for q in range(SLICES):
+            cols = slice(q * SLICE, (q + 1) * SLICE)
+            nc.vector.quantize_mx(
+                out=s_codes[:, cols].bitcast(FP8X4),
+                scales=s_scales[:, cols],
+                in_=grouped[:, cols, :].rearrange("p j t -> p (j t)"),
+            )
+            for b in range(BLOCKS):
+                nc.tensor.matmul_mx(
+                    out=banks[q][:, b, :],
+                    lhsT=w_codes[:, 2 * P * b : 2 * P * (b + 1)].bitcast(FP4X4),
+                    lhsT_scale=w_sc[:, P * b : P * (b + 1)],
+                    rhs=s_codes[:, cols].bitcast(FP8X4),
+                    rhs_scale=s_scales[:, cols],
+                    start=False,
+                    stop=(b == BLOCKS - 1),
+                )
+            result = keep.tile([P, BLOCKS, SLICE], F32, name="result%d" % q)
+            nc.scalar.activation(result[:], banks[q][:], SILU, scale=0.6)
+            nc.sync.dma_start(out_rows[:, :, cols], result[:])

@@ -1,6 +1,7 @@
 from contextlib import ExitStack
 
 import concourse.mybir as mybir
+from concourse.masks import make_identity
 
 K, T, J, L, N = 512, 1024, 512, 512, 512
 FLOPS = 2 * K * N * J + 2 * L * N * J
@@ -24,7 +25,7 @@ SLICE = 128
 SLICES = J // SLICE
 BLOCKS = N // P
 
-ORDER = [(0, 0), (0, 1), (1, 0), (1, 1), (2, 0), (0, 2), (2, 1), (1, 2), (0, 3), (2, 2), (1, 3), (2, 3)]
+ORDER = [(i, t) for t in range(PACK) for i in range(3)]
 
 
 def tile_list_three_tables_summed_kernel(
@@ -34,6 +35,8 @@ def tile_list_three_tables_summed_kernel(
     with ExitStack() as ctx:
         keep = ctx.enter_context(tc.tile_pool(name="keep", bufs=1))
         psum = ctx.enter_context(tc.psum_pool(name="psum", bufs=1))
+        turn = ctx.enter_context(tc.psum_pool(name="turn", bufs=1))
+        stage = ctx.enter_context(tc.tile_pool(name="stage", bufs=2))
 
         sources = [x.rearrange("(p t) c -> p t c", t=PACK) for x in (xa, xb, xc)]
         lists_in = [offs, offs2, offs3]
@@ -50,6 +53,12 @@ def tile_list_three_tables_summed_kernel(
         s_scales = keep.tile([P, J], U8, name="s_scales", align_bytes=64)
         w_sc, wd_sc, dx_sc = given_scales[:, 0, :], given_scales[:, 1, :], given_scales[:, 2, :]
 
+        warm_in = keep.tile([P, 1], F32, name="warm_in")
+        warm_out = keep.tile([P, 1], F32, name="warm_out")
+        nc.vector.memset(warm_in[:], 0.0)
+        nc.scalar.activation(warm_out[:], warm_in[:], SILU, scale=0.6)
+        ident = keep.tile([P, P], F32, name="ident")
+        make_identity(nc, ident[:])
         nc.vector.memset(given_scales[:].rearrange("p a n -> p (a n)").bitcast(U32), 0)
         scale_rows = [(a, src, q) for a, src in enumerate((w_scales, wd_scales, dx_scales)) for q in range(4)]
 
@@ -74,7 +83,7 @@ def tile_list_three_tables_summed_kernel(
 
         def gather(i, t, j0, j1):
             picked = planes[i, t][:].indirect(lists[i][:, j0 // LIST_ROWS : j1 // LIST_ROWS])
-            if i == 0:
+            if i == 0 or t < PACK - 1:
                 nc.vector.tensor_copy(sums[i, t][:, j0:j1], picked)
             else:
                 nc.vector.tensor_tensor(sums[i, t][:, j0:j1], picked, sums[i - 1, t][:, j0:j1], ADD)
@@ -84,12 +93,32 @@ def tile_list_three_tables_summed_kernel(
 
         banks = [psum.tile([P, BLOCKS, SLICE], F32, name="bank%d" % q) for q in range(SLICES)]
 
-        for i, t in ORDER[:-2]:
-            gather(i, t, 0, J)
-            if i == 2:
-                scale_and_group(t, 0, J)
-        gather(1, 3, 0, J // 2)
-        gather(1, 3, J // 2, J)
+        for t in range(PACK - 1):
+            added = [turn.tile([P, 2, P], F32, name="added%d" % h) for h in range(2)]
+            for i in range(3):
+                gather(i, t, 0, J)
+                for q in range(SLICES):
+                    nc.tensor.matmul(
+                        added[q // 2][:, q % 2, :],
+                        sums[i, t][:, q * SLICE : (q + 1) * SLICE],
+                        ident[:],
+                        start=(i == 0 and q % 2 == 0),
+                        stop=(i == 2 and q % 2 == 1),
+                        is_transpose=True,
+                    )
+            turned = stage.tile([P, SLICES, P], F32, name="turned")
+            for h in range(2):
+                nc.scalar.copy(turned[:, 2 * h : 2 * h + 2, :], added[h][:])
+            for h in range(2):
+                back = turn.tile([P, J // 2], F32, name="back%d" % h)
+                for u in range(2):
+                    nc.tensor.transpose(back[:, u * SLICE : (u + 1) * SLICE], turned[:, 2 * h + u, :], ident[:])
+                nc.scalar.activation(
+                    grouped[:, h * J // 2 : (h + 1) * J // 2, t], back[:], COPY, scale=factor[:, t : t + 1]
+                )
+        for i in range(2):
+            gather(i, 3, 0, J // 2)
+            gather(i, 3, J // 2, J)
 
         for q in range(SLICES):
             cols = slice(q * SLICE, (q + 1) * SLICE)

@@ -1,7 +1,6 @@
 from contextlib import ExitStack
 
 import concourse.mybir as mybir
-from concourse.masks import make_identity
 
 K, T, J, L, N = 512, 1024, 512, 512, 512
 FLOPS = 2 * K * N * J + 2 * L * N * J
@@ -25,7 +24,12 @@ SLICE = 128
 SLICES = J // SLICE
 BLOCKS = N // P
 
-ORDER = [(i, t) for t in range(PACK) for i in range(3)]
+LAST = PACK - 1
+EARLY = [(0, 0), (0, 1), (1, 0), (1, 1), (2, 0), (0, 2), (2, 1), (1, 2), (0, 3), (2, 2)]
+ORDER = EARLY + [(1, LAST), (2, LAST)]
+RING = 3
+PARTS = 2
+PART = BLOCKS // PARTS
 
 
 def tile_list_three_tables_summed_kernel(
@@ -34,15 +38,14 @@ def tile_list_three_tables_summed_kernel(
     nc = tc.nc
     with ExitStack() as ctx:
         keep = ctx.enter_context(tc.tile_pool(name="keep", bufs=1))
+        ring = ctx.enter_context(tc.tile_pool(name="ring", bufs=3))
         psum = ctx.enter_context(tc.psum_pool(name="psum", bufs=1))
-        turn = ctx.enter_context(tc.psum_pool(name="turn", bufs=1))
-        stage = ctx.enter_context(tc.tile_pool(name="stage", bufs=2))
 
         sources = [x.rearrange("(p t) c -> p t c", t=PACK) for x in (xa, xb, xc)]
         lists_in = [offs, offs2, offs3]
         lists = [keep.tile([P, J // LIST_ROWS], U16, name="list%d" % i) for i in range(3)]
         planes = {(i, t): keep.tile([P, T], F32, name="plane%d_%d" % (i, t)) for i, t in ORDER}
-        sums = {(i, t): keep.tile([P, J], F32, name="sum%d_%d" % (i, t)) for i, t in ORDER}
+        sums = {(i, t): keep.tile([P, J], F32, name="sum%d_%d" % (i, t)) for i, t in ORDER if (i, t) != (2, LAST)}
         factor = keep.tile([P, PACK], F32, name="factor")
         w_codes = keep.tile([P, 2 * N], U8, name="w_codes", align_bytes=64)
         wd_codes = keep.tile([P, 2 * N], U8, name="wd_codes", align_bytes=64)
@@ -57,104 +60,98 @@ def tile_list_three_tables_summed_kernel(
         warm_out = keep.tile([P, 1], F32, name="warm_out")
         nc.vector.memset(warm_in[:], 0.0)
         nc.scalar.activation(warm_out[:], warm_in[:], SILU, scale=0.6)
-        ident = keep.tile([P, P], F32, name="ident")
-        make_identity(nc, ident[:])
         nc.vector.memset(given_scales[:].rearrange("p a n -> p (a n)").bitcast(U32), 0)
-        scale_rows = [(a, src, q) for a, src in enumerate((w_scales, wd_scales, dx_scales)) for q in range(4)]
+        dx_in = dx_words[0].rearrange("p n t -> p (n t)").bitcast(I32)
 
+        def load_words(codes, words):
+            nc.sync.dma_start(codes[:].bitcast(I32), words[0].bitcast(I32))
+
+        def load_dx(j0, j1):
+            nc.sync.dma_start(dx_codes[:, j0:j1].bitcast(I32), dx_in[:, j0:j1])
+
+        def load_scale_rows(a, src, q):
+            nc.sync.dma_start(
+                given_scales[32 * q : 32 * q + 4, a, :].bitcast(I32), src[0, 4 * q : 4 * q + 4, :].bitcast(I32)
+            )
+
+        direct_rows = [(1, wd_scales, q) for q in range(4)] + [(2, dx_scales, q) for q in range(4)]
         for step, (i, t) in enumerate(ORDER):
             if step == len(ORDER) - 1:
-                nc.sync.dma_start(wd_codes[:].bitcast(I32), wd_words[0].bitcast(I32))
-                nc.sync.dma_start(
-                    dx_codes[:].bitcast(I32), dx_words[0].rearrange("p n t -> p (n t)").bitcast(I32)
-                )
+                load_words(wd_codes, wd_words)
+                load_scale_rows(*direct_rows.pop())
+                load_dx(0, J // 2)
             nc.sync.dma_start(planes[i, t][:], sources[i][:, t, :])
             if t == 0:
                 nc.sync.dma_start(lists[i][:], lists_in[i])
-            if (i, t) == (2, 0):
+            elif step == 1:
                 nc.sync.dma_start(factor[:], fk.rearrange("(p t) o -> p (t o)", t=PACK))
-            if step >= 5:
-                for a, src, q in scale_rows[2 * (step - 5) : 2 * (step - 4)]:
-                    nc.sync.dma_start(
-                        given_scales[32 * q : 32 * q + 4, a, :].bitcast(I32),
-                        src[0, 4 * q : 4 * q + 4, :].bitcast(I32),
-                    )
-        nc.sync.dma_start(w_codes[:].bitcast(I32), w_words[0].bitcast(I32))
+            elif direct_rows:
+                load_scale_rows(*direct_rows.pop())
+        load_dx(J // 2, J)
+        for q in range(4):
+            load_scale_rows(0, w_scales, q)
+        load_words(w_codes, w_words)
 
-        def gather(i, t, j0, j1):
-            picked = planes[i, t][:].indirect(lists[i][:, j0 // LIST_ROWS : j1 // LIST_ROWS])
-            if i == 0 or t < PACK - 1:
-                nc.vector.tensor_copy(sums[i, t][:, j0:j1], picked)
+        def gather(dst, i, t, cols, so_far=None):
+            picked = planes[i, t][:].indirect(lists[i][:, cols.start // LIST_ROWS : cols.stop // LIST_ROWS])
+            if so_far is None:
+                nc.vector.tensor_copy(dst, picked)
             else:
-                nc.vector.tensor_tensor(sums[i, t][:, j0:j1], picked, sums[i - 1, t][:, j0:j1], ADD)
+                nc.vector.tensor_tensor(dst, picked, so_far, ADD)
 
-        def scale_and_group(t, j0, j1):
-            nc.scalar.activation(grouped[:, j0:j1, t], sums[2, t][:, j0:j1], COPY, scale=factor[:, t : t + 1])
+        def scale_and_group(t, cols, total):
+            nc.scalar.activation(grouped[:, cols, t], total, COPY, scale=factor[:, t : t + 1])
 
-        banks = [psum.tile([P, BLOCKS, SLICE], F32, name="bank%d" % q) for q in range(SLICES)]
-
-        for t in range(PACK - 1):
-            added = [turn.tile([P, 2, P], F32, name="added%d" % h) for h in range(2)]
-            for i in range(3):
-                gather(i, t, 0, J)
-                for q in range(SLICES):
-                    nc.tensor.matmul(
-                        added[q // 2][:, q % 2, :],
-                        sums[i, t][:, q * SLICE : (q + 1) * SLICE],
-                        ident[:],
-                        start=(i == 0 and q % 2 == 0),
-                        stop=(i == 2 and q % 2 == 1),
-                        is_transpose=True,
-                    )
-            turned = stage.tile([P, SLICES, P], F32, name="turned")
-            for h in range(2):
-                nc.scalar.copy(turned[:, 2 * h : 2 * h + 2, :], added[h][:])
-            for h in range(2):
-                back = turn.tile([P, J // 2], F32, name="back%d" % h)
-                for u in range(2):
-                    nc.tensor.transpose(back[:, u * SLICE : (u + 1) * SLICE], turned[:, 2 * h + u, :], ident[:])
-                nc.scalar.activation(
-                    grouped[:, h * J // 2 : (h + 1) * J // 2, t], back[:], COPY, scale=factor[:, t : t + 1]
-                )
-        for i in range(2):
-            gather(i, 3, 0, J // 2)
-            gather(i, 3, J // 2, J)
-
-        for q in range(SLICES):
-            cols = slice(q * SLICE, (q + 1) * SLICE)
-            for b in range(BLOCKS):
-                nc.tensor.matmul_mx(
-                    out=banks[q][:, b, :],
-                    lhsT=wd_codes[:, 2 * P * b : 2 * P * (b + 1)].bitcast(FP4X4),
-                    lhsT_scale=wd_sc[:, P * b : P * (b + 1)],
-                    rhs=dx_codes[:, cols].bitcast(FP8X4),
-                    rhs_scale=dx_sc[:, cols],
-                    start=(b == 0),
-                    stop=False,
-                )
-
-        for q in range(SLICES):
-            gather(2, 3, q * SLICE, (q + 1) * SLICE)
-            scale_and_group(3, q * SLICE, (q + 1) * SLICE)
+        def product(bank, codes, scales, b, rhs, rhs_scale, start, stop):
+            nc.tensor.matmul_mx(
+                out=bank,
+                lhsT=codes[:, 2 * P * b : 2 * P * (b + 1)].bitcast(FP4X4),
+                lhsT_scale=scales[:, P * b : P * (b + 1)],
+                rhs=rhs.bitcast(FP8X4),
+                rhs_scale=rhs_scale,
+                start=start,
+                stop=stop,
+            )
 
         out_rows = out.rearrange("(b p) j -> p b j", p=P)
-        for q in range(SLICES):
+
+        def finish(q):
             cols = slice(q * SLICE, (q + 1) * SLICE)
             nc.vector.quantize_mx(
                 out=s_codes[:, cols].bitcast(FP8X4),
                 scales=s_scales[:, cols],
                 in_=grouped[:, cols, :].rearrange("p j t -> p (j t)"),
             )
-            for b in range(BLOCKS):
-                nc.tensor.matmul_mx(
-                    out=banks[q][:, b, :],
-                    lhsT=w_codes[:, 2 * P * b : 2 * P * (b + 1)].bitcast(FP4X4),
-                    lhsT_scale=w_sc[:, P * b : P * (b + 1)],
-                    rhs=s_codes[:, cols].bitcast(FP8X4),
-                    rhs_scale=s_scales[:, cols],
-                    start=False,
-                    stop=(b == BLOCKS - 1),
-                )
-            result = keep.tile([P, BLOCKS, SLICE], F32, name="result%d" % q)
-            nc.scalar.activation(result[:], banks[q][:], SILU, scale=0.6)
-            nc.sync.dma_start(out_rows[:, :, cols], result[:])
+            for part in range(PARTS):
+                bank = banks[q, part]
+                for u in range(PART):
+                    product(bank[:, u, :], w_codes, w_sc, part * PART + u, s_codes[:, cols], s_scales[:, cols], False, u == PART - 1)
+                result = keep.tile([P, PART, SLICE], F32, name="result%d_%d" % (q, part))
+                nc.scalar.activation(result[:], bank[:], SILU, scale=0.6)
+                nc.sync.dma_start(out_rows[:, part * PART : (part + 1) * PART, cols], result[:])
+
+        banks = {}
+        for q in range(SLICES):
+            cols = slice(q * SLICE, (q + 1) * SLICE)
+            for part in range(PARTS):
+                banks[q, part] = psum.tile([P, PART, SLICE], F32, name="bank%d_%d" % (q, part))
+                for u in range(PART):
+                    product(banks[q, part][:, u, :], wd_codes, wd_sc, part * PART + u, dx_codes[:, cols], dx_sc[:, cols], u == 0, False)
+
+        whole = slice(0, J)
+        for i, t in EARLY:
+            gather(sums[i, t][:], i, t, whole, sums[i - 1, t][:] if i else None)
+            if i == 2:
+                scale_and_group(t, whole, sums[i, t][:])
+        for h in range(2):
+            cols = slice(h * J // 2, (h + 1) * J // 2)
+            gather(sums[1, LAST][:, cols], 1, LAST, cols, sums[0, LAST][:, cols])
+
+        for q in range(SLICES + RING):
+            if q >= RING:
+                finish(q - RING)
+            if q < SLICES:
+                cols = slice(q * SLICE, (q + 1) * SLICE)
+                total = ring.tile([P, SLICE], F32, name="total")
+                gather(total[:], 2, LAST, cols, sums[1, LAST][:, cols])
+                scale_and_group(LAST, cols, total[:])

@@ -25,8 +25,8 @@ SLICES = J // SLICE
 BLOCKS = N // P
 
 LAST = PACK - 1
-EARLY = [(0, 0), (0, 1), (1, 0), (1, 1), (2, 0), (0, 2), (2, 1), (1, 2), (0, 3), (2, 2)]
-ORDER = EARLY + [(1, LAST), (2, LAST)]
+EARLY = [(0, 0), (0, 1), (1, 0), (0, 2), (2, 0), (1, 1), (1, 2), (2, 1), (2, 2)]
+ORDER = EARLY + [(0, LAST), (1, LAST), (2, LAST)]
 RING = 3
 PARTS = 2
 PART = BLOCKS // PARTS
@@ -77,9 +77,7 @@ def tile_list_three_tables_summed_kernel(
         direct_rows = [(1, wd_scales, q) for q in range(4)] + [(2, dx_scales, q) for q in range(4)]
         for step, (i, t) in enumerate(ORDER):
             if step == len(ORDER) - 1:
-                load_words(wd_codes, wd_words)
                 load_scale_rows(*direct_rows.pop())
-                load_dx(0, J // 2)
             nc.sync.dma_start(planes[i, t][:], sources[i][:, t, :])
             if t == 0:
                 nc.sync.dma_start(lists[i][:], lists_in[i])
@@ -87,10 +85,12 @@ def tile_list_three_tables_summed_kernel(
                 nc.sync.dma_start(factor[:], fk.rearrange("(p t) o -> p (t o)", t=PACK))
             elif direct_rows:
                 load_scale_rows(*direct_rows.pop())
-        load_dx(J // 2, J)
+        load_words(wd_codes, wd_words)
+        load_dx(0, J // 2)
         for q in range(4):
             load_scale_rows(0, w_scales, q)
         load_words(w_codes, w_words)
+        load_dx(J // 2, J)
 
         def gather(dst, i, t, cols, so_far=None):
             picked = planes[i, t][:].indirect(lists[i][:, cols.start // LIST_ROWS : cols.stop // LIST_ROWS])
@@ -115,6 +115,8 @@ def tile_list_three_tables_summed_kernel(
 
         out_rows = out.rearrange("(b p) j -> p b j", p=P)
 
+        banks = {}
+
         def finish(q):
             cols = slice(q * SLICE, (q + 1) * SLICE)
             nc.vector.quantize_mx(
@@ -130,25 +132,29 @@ def tile_list_three_tables_summed_kernel(
                 nc.scalar.activation(result[:], bank[:], SILU, scale=0.6)
                 nc.sync.dma_start(out_rows[:, part * PART : (part + 1) * PART, cols], result[:])
 
-        banks = {}
-        for q in range(SLICES):
+        def direct(q):
             cols = slice(q * SLICE, (q + 1) * SLICE)
             for part in range(PARTS):
                 banks[q, part] = psum.tile([P, PART, SLICE], F32, name="bank%d_%d" % (q, part))
                 for u in range(PART):
                     product(banks[q, part][:, u, :], wd_codes, wd_sc, part * PART + u, dx_codes[:, cols], dx_sc[:, cols], u == 0, False)
 
+        direct(0)
+        direct(1)
         whole = slice(0, J)
         for i, t in EARLY:
             gather(sums[i, t][:], i, t, whole, sums[i - 1, t][:] if i else None)
             if i == 2:
                 scale_and_group(t, whole, sums[i, t][:])
-        for h in range(2):
-            cols = slice(h * J // 2, (h + 1) * J // 2)
-            gather(sums[1, LAST][:, cols], 1, LAST, cols, sums[0, LAST][:, cols])
+        for i in range(2):
+            for h in range(2):
+                cols = slice(h * J // 2, (h + 1) * J // 2)
+                gather(sums[i, LAST][:, cols], i, LAST, cols, sums[0, LAST][:, cols] if i else None)
 
         for q in range(SLICES + RING):
             if q >= RING:
+                if q - RING >= 2:
+                    direct(q - RING)
                 finish(q - RING)
             if q < SLICES:
                 cols = slice(q * SLICE, (q + 1) * SLICE)

@@ -19,17 +19,18 @@ SILU = mybir.ActivationFunctionType.Silu
 
 P = 128
 PACK = 4
+TABLES = 3
 LIST_ROWS = 16
+QUADRANTS = 4
 SLICE = 128
-SLICES = J // SLICE
+HALF = J // 2
 BLOCKS = N // P
+GAIN = 0.6
+W_SC, WD_SC, DX_SC = 0, 1, 2
 
 LAST = PACK - 1
-EARLY = [(0, 0), (0, 1), (1, 0), (0, 2), (2, 0), (1, 1), (1, 2), (2, 1), (2, 2)]
-ORDER = EARLY + [(0, LAST), (1, LAST), (2, LAST)]
-RING = 3
-PARTS = 2
-PART = BLOCKS // PARTS
+EARLY = sorted(((i, t) for i in range(TABLES) for t in range(LAST)), key=lambda it: (it[0] + it[1], it[0]))
+ORDER = EARLY + [(i, LAST) for i in range(TABLES)]
 
 
 def tile_list_three_tables_summed_kernel(
@@ -38,14 +39,13 @@ def tile_list_three_tables_summed_kernel(
     nc = tc.nc
     with ExitStack() as ctx:
         keep = ctx.enter_context(tc.tile_pool(name="keep", bufs=1))
-        ring = ctx.enter_context(tc.tile_pool(name="ring", bufs=3))
         psum = ctx.enter_context(tc.psum_pool(name="psum", bufs=1))
 
-        sources = [x.rearrange("(p t) c -> p t c", t=PACK) for x in (xa, xb, xc)]
-        lists_in = [offs, offs2, offs3]
-        lists = [keep.tile([P, J // LIST_ROWS], U16, name="list%d" % i) for i in range(3)]
+        tables = [x.rearrange("(p t) c -> p t c", t=PACK) for x in (xa, xb, xc)]
+        lists_hbm = [offs, offs2, offs3]
+        lists = [keep.tile([P, J // LIST_ROWS], U16, name="list%d" % i) for i in range(TABLES)]
         planes = {(i, t): keep.tile([P, T], F32, name="plane%d_%d" % (i, t)) for i, t in ORDER}
-        sums = {(i, t): keep.tile([P, J], F32, name="sum%d_%d" % (i, t)) for i, t in ORDER if (i, t) != (2, LAST)}
+        sums = {(i, t): keep.tile([P, J], F32, name="sum%d_%d" % (i, t)) for i, t in ORDER}
         factor = keep.tile([P, PACK], F32, name="factor")
         w_codes = keep.tile([P, 2 * N], U8, name="w_codes", align_bytes=64)
         wd_codes = keep.tile([P, 2 * N], U8, name="wd_codes", align_bytes=64)
@@ -54,110 +54,106 @@ def tile_list_three_tables_summed_kernel(
         grouped = keep.tile([P, J, PACK], BF16, name="grouped", align_bytes=64)
         s_codes = keep.tile([P, J], U32, name="s_codes", align_bytes=64)
         s_scales = keep.tile([P, J], U8, name="s_scales", align_bytes=64)
-        w_sc, wd_sc, dx_sc = given_scales[:, 0, :], given_scales[:, 1, :], given_scales[:, 2, :]
 
         warm_in = keep.tile([P, 1], F32, name="warm_in")
         warm_out = keep.tile([P, 1], F32, name="warm_out")
         nc.vector.memset(warm_in[:], 0.0)
-        nc.scalar.activation(warm_out[:], warm_in[:], SILU, scale=0.6)
+        nc.scalar.activation(warm_out[:], warm_in[:], SILU, scale=GAIN)
+
         nc.vector.memset(given_scales[:].rearrange("p a n -> p (a n)").bitcast(U32), 0)
-        dx_in = dx_words[0].rearrange("p n t -> p (n t)").bitcast(I32)
+
+        dx_hbm = dx_words[0].rearrange("p n t -> p (n t)").bitcast(I32)
 
         def load_words(codes, words):
             nc.sync.dma_start(codes[:].bitcast(I32), words[0].bitcast(I32))
 
-        def load_dx(j0, j1):
-            nc.sync.dma_start(dx_codes[:, j0:j1].bitcast(I32), dx_in[:, j0:j1])
+        def load_dx(h):
+            cols = slice(h * HALF, (h + 1) * HALF)
+            nc.sync.dma_start(dx_codes[:, cols].bitcast(I32), dx_hbm[:, cols])
 
-        def load_scale_rows(a, src, q):
+        def load_scale_rows(place, scales, quadrant):
             nc.sync.dma_start(
-                given_scales[32 * q : 32 * q + 4, a, :].bitcast(I32), src[0, 4 * q : 4 * q + 4, :].bitcast(I32)
+                given_scales[32 * quadrant : 32 * quadrant + 4, place, :].bitcast(I32),
+                scales[0, 4 * quadrant : 4 * quadrant + 4, :].bitcast(I32),
             )
 
-        direct_rows = [(1, wd_scales, q) for q in range(4)] + [(2, dx_scales, q) for q in range(4)]
+        direct_rows = [(WD_SC, wd_scales, q) for q in range(QUADRANTS)]
+        direct_rows.extend((DX_SC, dx_scales, q) for q in range(QUADRANTS))
         for step, (i, t) in enumerate(ORDER):
             if step == len(ORDER) - 1:
                 load_scale_rows(*direct_rows.pop())
-            nc.sync.dma_start(planes[i, t][:], sources[i][:, t, :])
+            nc.sync.dma_start(planes[i, t][:], tables[i][:, t, :])
             if t == 0:
-                nc.sync.dma_start(lists[i][:], lists_in[i])
+                nc.sync.dma_start(lists[i][:], lists_hbm[i])
             elif step == 1:
                 nc.sync.dma_start(factor[:], fk.rearrange("(p t) o -> p (t o)", t=PACK))
             elif direct_rows:
                 load_scale_rows(*direct_rows.pop())
         load_words(wd_codes, wd_words)
-        load_dx(0, J // 2)
-        for q in range(4):
-            load_scale_rows(0, w_scales, q)
+        load_dx(0)
+        for q in range(QUADRANTS):
+            load_scale_rows(W_SC, w_scales, q)
         load_words(w_codes, w_words)
-        load_dx(J // 2, J)
+        load_dx(1)
 
-        def gather(dst, i, t, cols, so_far=None):
+        def gather(i, t, cols):
             picked = planes[i, t][:].indirect(lists[i][:, cols.start // LIST_ROWS : cols.stop // LIST_ROWS])
-            if so_far is None:
-                nc.vector.tensor_copy(dst, picked)
+            if i == 0:
+                nc.vector.tensor_copy(sums[i, t][:, cols], picked)
             else:
-                nc.vector.tensor_tensor(dst, picked, so_far, ADD)
+                nc.vector.tensor_tensor(sums[i, t][:, cols], picked, sums[i - 1, t][:, cols], ADD)
 
-        def scale_and_group(t, cols, total):
-            nc.scalar.activation(grouped[:, cols, t], total, COPY, scale=factor[:, t : t + 1])
-
-        def product(bank, codes, scales, b, rhs, rhs_scale, start, stop):
-            nc.tensor.matmul_mx(
-                out=bank,
-                lhsT=codes[:, 2 * P * b : 2 * P * (b + 1)].bitcast(FP4X4),
-                lhsT_scale=scales[:, P * b : P * (b + 1)],
-                rhs=rhs.bitcast(FP8X4),
-                rhs_scale=rhs_scale,
-                start=start,
-                stop=stop,
-            )
-
-        out_rows = out.rearrange("(b p) j -> p b j", p=P)
+        def scale_and_group(t, cols):
+            nc.scalar.activation(grouped[:, cols, t], sums[TABLES - 1, t][:, cols], COPY, scale=factor[:, t : t + 1])
 
         banks = {}
 
-        def finish(q):
-            cols = slice(q * SLICE, (q + 1) * SLICE)
+        def passes(h, b, weight_codes, weight_place, moving_codes, moving_scales, opens):
+            for u in range(HALF // SLICE):
+                cols = slice(h * HALF + u * SLICE, h * HALF + (u + 1) * SLICE)
+                nc.tensor.matmul_mx(
+                    out=banks[h, b][:, u * SLICE : (u + 1) * SLICE],
+                    lhsT=weight_codes[:, 2 * P * b : 2 * P * (b + 1)].bitcast(FP4X4),
+                    lhsT_scale=given_scales[:, weight_place, P * b : P * (b + 1)],
+                    rhs=moving_codes[:, cols].bitcast(FP8X4),
+                    rhs_scale=moving_scales[:, cols],
+                    start=opens and u == 0,
+                    stop=not opens and u == HALF // SLICE - 1,
+                )
+
+        def direct(h, b):
+            banks[h, b] = psum.tile([P, HALF], F32, name="bank%d_%d" % (h, b))
+            passes(h, b, wd_codes, WD_SC, dx_codes, given_scales[:, DX_SC, :], True)
+
+        def finish(h, b):
+            passes(h, b, w_codes, W_SC, s_codes, s_scales, False)
+            result = keep.tile([P, HALF], F32, name="result%d_%d" % (h, b))
+            nc.scalar.activation(result[:], banks[h, b][:], SILU, scale=GAIN)
+            nc.sync.dma_start(out[b * P : (b + 1) * P, h * HALF : (h + 1) * HALF], result[:])
+
+        for b in range(BLOCKS):
+            direct(0, b)
+
+        for i, t in EARLY:
+            gather(i, t, slice(0, J))
+            if i == TABLES - 1:
+                scale_and_group(t, slice(0, J))
+
+        for i in range(TABLES - 1):
+            for h in range(J // HALF):
+                gather(i, LAST, slice(h * HALF, (h + 1) * HALF))
+        for j0 in range(0, J, SLICE):
+            gather(TABLES - 1, LAST, slice(j0, j0 + SLICE))
+            scale_and_group(LAST, slice(j0, j0 + SLICE))
+
+        for h in range(J // HALF):
+            cols = slice(h * HALF, (h + 1) * HALF)
             nc.vector.quantize_mx(
                 out=s_codes[:, cols].bitcast(FP8X4),
                 scales=s_scales[:, cols],
                 in_=grouped[:, cols, :].rearrange("p j t -> p (j t)"),
             )
-            for part in range(PARTS):
-                bank = banks[q, part]
-                for u in range(PART):
-                    product(bank[:, u, :], w_codes, w_sc, part * PART + u, s_codes[:, cols], s_scales[:, cols], False, u == PART - 1)
-                result = keep.tile([P, PART, SLICE], F32, name="result%d_%d" % (q, part))
-                nc.scalar.activation(result[:], bank[:], SILU, scale=0.6)
-                nc.sync.dma_start(out_rows[:, part * PART : (part + 1) * PART, cols], result[:])
-
-        def direct(q):
-            cols = slice(q * SLICE, (q + 1) * SLICE)
-            for part in range(PARTS):
-                banks[q, part] = psum.tile([P, PART, SLICE], F32, name="bank%d_%d" % (q, part))
-                for u in range(PART):
-                    product(banks[q, part][:, u, :], wd_codes, wd_sc, part * PART + u, dx_codes[:, cols], dx_sc[:, cols], u == 0, False)
-
-        direct(0)
-        direct(1)
-        whole = slice(0, J)
-        for i, t in EARLY:
-            gather(sums[i, t][:], i, t, whole, sums[i - 1, t][:] if i else None)
-            if i == 2:
-                scale_and_group(t, whole, sums[i, t][:])
-        for i in range(2):
-            for h in range(2):
-                cols = slice(h * J // 2, (h + 1) * J // 2)
-                gather(sums[i, LAST][:, cols], i, LAST, cols, sums[0, LAST][:, cols] if i else None)
-
-        for q in range(SLICES + RING):
-            if q >= RING:
-                if q - RING >= 2:
-                    direct(q - RING)
-                finish(q - RING)
-            if q < SLICES:
-                cols = slice(q * SLICE, (q + 1) * SLICE)
-                total = ring.tile([P, SLICE], F32, name="total")
-                gather(total[:], 2, LAST, cols, sums[1, LAST][:, cols])
-                scale_and_group(LAST, cols, total[:])
+            for b in range(BLOCKS):
+                if h > 0:
+                    direct(h, b)
+                finish(h, b)

from contextlib import ExitStack

import concourse.mybir as mybir

K, T, J, L, N = 512, 1024, 512, 512, 512
FLOPS = 2 * K * N * J + 2 * L * N * J

F32 = mybir.dt.float32
BF16 = mybir.dt.bfloat16
I32 = mybir.dt.int32
U32 = mybir.dt.uint32
U16 = mybir.dt.uint16
U8 = mybir.dt.uint8
FP8X4 = mybir.dt.float8_e4m3fn_x4
FP4X4 = mybir.dt.float4_e2m1fn_x4
ADD = mybir.AluOpType.add
COPY = mybir.ActivationFunctionType.Copy
SILU = mybir.ActivationFunctionType.Silu

P = 128
PACK = 4
TABLES = 3
LIST_ROWS = 16
QUADRANTS = 4
SLICE = 128
HALF = J // 2
BLOCKS = N // P
GAIN = 0.6
W_SC, WD_SC, DX_SC = 0, 1, 2

LAST = PACK - 1
EARLY = sorted(((i, t) for i in range(TABLES) for t in range(LAST)), key=lambda it: (it[0] + it[1], it[0]))
ORDER = EARLY + [(i, LAST) for i in range(TABLES)]


def tile_list_three_tables_summed_kernel(
    tc, xa, xb, xc, fk, w_words, w_scales, dx_words, dx_scales, wd_words, wd_scales, offs, offs2, offs3, out
):
    nc = tc.nc
    with ExitStack() as ctx:
        keep = ctx.enter_context(tc.tile_pool(name="keep", bufs=1))
        psum = ctx.enter_context(tc.psum_pool(name="psum", bufs=1))

        tables = [x.rearrange("(p t) c -> p t c", t=PACK) for x in (xa, xb, xc)]
        lists_hbm = [offs, offs2, offs3]
        lists = [keep.tile([P, J // LIST_ROWS], U16, name="list%d" % i) for i in range(TABLES)]
        planes = {(i, t): keep.tile([P, T], F32, name="plane%d_%d" % (i, t)) for i, t in ORDER}
        sums = {(i, t): keep.tile([P, J], F32, name="sum%d_%d" % (i, t)) for i, t in ORDER}
        factor = keep.tile([P, PACK], F32, name="factor")
        w_codes = keep.tile([P, 2 * N], U8, name="w_codes", align_bytes=64)
        wd_codes = keep.tile([P, 2 * N], U8, name="wd_codes", align_bytes=64)
        dx_codes = keep.tile([P, J], U32, name="dx_codes", align_bytes=64)
        given_scales = keep.tile([P, 3, N], U8, name="given_scales", align_bytes=64)
        grouped = keep.tile([P, J, PACK], BF16, name="grouped", align_bytes=64)
        s_codes = keep.tile([P, J], U32, name="s_codes", align_bytes=64)
        s_scales = keep.tile([P, J], U8, name="s_scales", align_bytes=64)

        warm_in = keep.tile([P, 1], F32, name="warm_in")
        warm_out = keep.tile([P, 1], F32, name="warm_out")
        nc.vector.memset(warm_in[:], 0.0)
        nc.scalar.activation(warm_out[:], warm_in[:], SILU, scale=GAIN)

        nc.vector.memset(given_scales[:].rearrange("p a n -> p (a n)").bitcast(U32), 0)

        dx_hbm = dx_words[0].rearrange("p n t -> p (n t)").bitcast(I32)

        def load_words(codes, words):
            nc.sync.dma_start(codes[:].bitcast(I32), words[0].bitcast(I32))

        def load_dx(h):
            cols = slice(h * HALF, (h + 1) * HALF)
            nc.sync.dma_start(dx_codes[:, cols].bitcast(I32), dx_hbm[:, cols])

        def load_scale_rows(place, scales, quadrant):
            nc.sync.dma_start(
                given_scales[32 * quadrant : 32 * quadrant + 4, place, :].bitcast(I32),
                scales[0, 4 * quadrant : 4 * quadrant + 4, :].bitcast(I32),
            )

        direct_rows = [(WD_SC, wd_scales, q) for q in range(QUADRANTS)]
        direct_rows.extend((DX_SC, dx_scales, q) for q in range(QUADRANTS))
        for step, (i, t) in enumerate(ORDER):
            if step == len(ORDER) - 1:
                load_scale_rows(*direct_rows.pop())
            nc.sync.dma_start(planes[i, t][:], tables[i][:, t, :])
            if t == 0:
                nc.sync.dma_start(lists[i][:], lists_hbm[i])
            elif step == 1:
                nc.sync.dma_start(factor[:], fk.rearrange("(p t) o -> p (t o)", t=PACK))
            elif direct_rows:
                load_scale_rows(*direct_rows.pop())
        load_words(wd_codes, wd_words)
        load_dx(0)
        for q in range(QUADRANTS):
            load_scale_rows(W_SC, w_scales, q)
        load_words(w_codes, w_words)
        load_dx(1)

        def gather(i, t, cols):
            picked = planes[i, t][:].indirect(lists[i][:, cols.start // LIST_ROWS : cols.stop // LIST_ROWS])
            if i == 0:
                nc.vector.tensor_copy(sums[i, t][:, cols], picked)
            else:
                nc.vector.tensor_tensor(sums[i, t][:, cols], picked, sums[i - 1, t][:, cols], ADD)

        def scale_and_group(t, cols):
            nc.scalar.activation(grouped[:, cols, t], sums[TABLES - 1, t][:, cols], COPY, scale=factor[:, t : t + 1])

        banks = {}

        def passes(h, b, weight_codes, weight_place, moving_codes, moving_scales, opens):
            for u in range(HALF // SLICE):
                cols = slice(h * HALF + u * SLICE, h * HALF + (u + 1) * SLICE)
                nc.tensor.matmul_mx(
                    out=banks[h, b][:, u * SLICE : (u + 1) * SLICE],
                    lhsT=weight_codes[:, 2 * P * b : 2 * P * (b + 1)].bitcast(FP4X4),
                    lhsT_scale=given_scales[:, weight_place, P * b : P * (b + 1)],
                    rhs=moving_codes[:, cols].bitcast(FP8X4),
                    rhs_scale=moving_scales[:, cols],
                    start=opens and u == 0,
                    stop=not opens and u == HALF // SLICE - 1,
                )

        def direct(h, b):
            banks[h, b] = psum.tile([P, HALF], F32, name="bank%d_%d" % (h, b))
            passes(h, b, wd_codes, WD_SC, dx_codes, given_scales[:, DX_SC, :], True)

        def finish(h, b):
            passes(h, b, w_codes, W_SC, s_codes, s_scales, False)
            result = keep.tile([P, HALF], F32, name="result%d_%d" % (h, b))
            nc.scalar.activation(result[:], banks[h, b][:], SILU, scale=GAIN)
            nc.sync.dma_start(out[b * P : (b + 1) * P, h * HALF : (h + 1) * HALF], result[:])

        for b in range(BLOCKS):
            direct(0, b)

        for i, t in EARLY:
            gather(i, t, slice(0, J))
            if i == TABLES - 1:
                scale_and_group(t, slice(0, J))

        for i in range(TABLES - 1):
            for h in range(J // HALF):
                gather(i, LAST, slice(h * HALF, (h + 1) * HALF))
        for j0 in range(0, J, SLICE):
            gather(TABLES - 1, LAST, slice(j0, j0 + SLICE))
            scale_and_group(LAST, slice(j0, j0 + SLICE))

        for h in range(J // HALF):
            cols = slice(h * HALF, (h + 1) * HALF)
            nc.vector.quantize_mx(
                out=s_codes[:, cols].bitcast(FP8X4),
                scales=s_scales[:, cols],
                in_=grouped[:, cols, :].rearrange("p j t -> p (j t)"),
            )
            for b in range(BLOCKS):
                if h > 0:
                    direct(h, b)
                finish(h, b)
